import numpy as np
import ml_dtypes


def mxq(x, axis, fmt="e4m3"):
    dtype, down = {"e4m3": (ml_dtypes.float8_e4m3fn, 7), "e5m2": (ml_dtypes.float8_e5m2, 14)}[fmt]
    v = np.moveaxis(np.asarray(x, np.float32).astype(ml_dtypes.bfloat16).astype(np.float64), axis, -1)
    blocks = v.reshape(v.shape[:-1] + (-1, 32))
    amax = np.abs(blocks).max(-1, keepdims=True)
    byte = np.maximum(np.where(amax > 0, np.frexp(amax)[1] - 1 + 127, 0) - down, 1)
    scale = np.exp2(byte - 127.0)
    codes = (blocks / scale).astype(np.float32).astype(dtype).astype(np.float64)
    return np.moveaxis((codes * scale).reshape(v.shape), -1, axis)


WIDE = False


def mx_kscale(k):
    if not WIDE:
        return np.ones(k)
    levels = np.array([10, -10, 5, -5, 0])
    if k % 512:
        return np.exp2(np.random.permutation(np.resize(levels, k // 32))).repeat(32)
    a = np.empty((k // 512, 16))
    for p in range(k // 512):
        a[p, :8] = np.random.permutation(np.resize(levels, 8))
        for g in range(8):
            far = levels[np.abs(levels - a[p, g]) >= 10]
            a[p, g + 8] = far[np.random.randint(len(far))]
    return np.exp2(a.ravel()).repeat(32)


def f64(x):
    return np.asarray(x).astype(np.float64)


def striped(idx):
    return np.tile(idx.reshape(-1, 16).T, (8, 1)).astype(np.uint16)


def unstriped(offs):
    return offs[:16].T.reshape(-1).astype(np.int64)

def planes(y):
    n, m = y.shape
    v = y.astype(np.float32).astype(ml_dtypes.bfloat16).astype(np.float64).reshape(n // 32, 32, m)
    top = np.abs(v).max(1)
    byte = np.clip(np.where(top > 0, np.frexp(top)[1] - 1 + 127 - 7, 1), 1, 254)
    codes = (v * np.exp2(127.0 - byte)[:, None, :]).reshape(n, m).astype(np.float32).astype(ml_dtypes.float8_e4m3fn).view(np.uint8)
    words = codes.reshape(n // 512, 128, 4, m).transpose(0, 1, 3, 2)
    return np.ascontiguousarray(words), np.ascontiguousarray(byte.astype(np.uint8).reshape(n // 512, 16, m))


K, T, S, V, N = 512, 1024, 512, 128, 512


def setup_inputs():
    n = np.random.standard_normal
    s = mx_kscale(K)[:, None]
    return {
        "xT": (n((K, T)) * s).astype(np.float32),
        "w1": (n((K, N)) / np.sqrt(K) / s).astype(np.float32),
        "w2": (n((K, N)) / np.sqrt(K) / s).astype(np.float32),
        "offs": striped(np.random.permutation(T)[:S]),
    }


def reference(xT, w1, w2, offs):
    xq = mxq(f64(xT)[:, unstriped(offs)], 0, "e4m3")
    e = np.exp(mxq(f64(w1), 0, "e4m3").T @ xq)
    h = mxq(f64(w2), 0, "e4m3").T @ xq
    num = e[:, :V] * h[:, :V] + e[:, V:2 * V] * h[:, V:2 * V] + e[:, 2 * V:3 * V] * h[:, 2 * V:3 * V] + e[:, 3 * V:4 * V] * h[:, 3 * V:4 * V]
    den = e[:, :V] + e[:, V:2 * V] + e[:, 2 * V:3 * V] + e[:, 3 * V:4 * V]
    out_0 = num / den
    return (out_0,) + planes(out_0)

@@ -1,0 +1,186 @@
+from contextlib import ExitStack
+
+import concourse.mybir as mybir
+from concourse.masks import make_identity
+
+K, T, S, V, N = 512, 1024, 512, 128, 512
+D = S // V
+P = 128
+PACK = 4
+
+FLOPS = 2 * 2 * K * N * S
+
+F32 = mybir.dt.float32
+BF16 = mybir.dt.bfloat16
+I32 = mybir.dt.int32
+U32 = mybir.dt.uint32
+U16 = mybir.dt.uint16
+U8 = mybir.dt.uint8
+FP8X4 = mybir.dt.float8_e4m3fn_x4
+ACT = mybir.ActivationFunctionType
+ALU = mybir.AluOpType
+AXIS = mybir.AxisListType
+
+
+def tile_picked_apool_none_lo_kernel(tc, xT, w1, w2, offs, out_0, out_1, out_2):
+    nc = tc.nc
+    with ExitStack() as ctx:
+        keep = ctx.enter_context(tc.tile_pool(name="keep", bufs=1))
+        psum = ctx.enter_context(tc.psum_pool(name="psum", bufs=1))
+
+        offsets = keep.tile([P, S // 16], U16, name="offsets")
+        x_rows = xT.rearrange("(p j) t -> p j t", j=PACK)
+        x_plane = [keep.tile([P, T], F32, name="x_plane%d" % j) for j in range(PACK)]
+        nc.sync.dma_start(out=x_plane[0][:], in_=x_rows[:, 0, :])
+        nc.sync.dma_start(offsets[:], offs)
+        for j in range(1, PACK):
+            nc.sync.dma_start(out=x_plane[j][:], in_=x_rows[:, j, :])
+
+        w1_raw = keep.tile([P, PACK, N], F32, name="w1_raw")
+        nc.sync.dma_start(out=w1_raw[:], in_=w1.rearrange("(p j) n -> p j n", j=PACK))
+        w2_raw = keep.tile([P, PACK, N], F32, name="w2_raw")
+        nc.sync.dma_start(out=w2_raw[:], in_=w2.rearrange("(p j) n -> p j n", j=PACK))
+
+        ident = keep.tile([P, P], F32, name="ident")
+        make_identity(nc, ident[:])
+
+        picked = keep.tile([P, PACK, S], BF16, name="picked")
+        for j in range(PACK):
+            nc.vector.tensor_copy(picked[:, j, :], x_plane[j][:].indirect(offsets[:]))
+        x_grouped = keep.tile([P, S, PACK], BF16, name="x_grouped", align_bytes=64)
+        nc.scalar.activation(
+            out=x_grouped[:, :, 0:2],
+            in_=picked[:, 0:2, :].rearrange("p j c -> p c j"),
+            func=ACT.Copy,
+        )
+        nc.vector.tensor_copy(out=x_grouped[:, :, 2:4], in_=picked[:, 2:4, :].rearrange("p j c -> p c j"))
+        x_codes = keep.tile([P, S], U32, name="x_codes", align_bytes=64)
+        x_scales = keep.tile([P, S], U8, name="x_scales", align_bytes=64)
+        nc.vector.quantize_mx(
+            out=x_codes[:].bitcast(FP8X4), scales=x_scales[:], in_=x_grouped[:].rearrange("p c j -> p (c j)")
+        )
+
+        def quantize(codes, scales, grouped, a, b):
+            nc.vector.quantize_mx(
+                out=codes[:, a:b].bitcast(FP8X4), scales=scales[:, a:b], in_=grouped[:, a * PACK : b * PACK]
+            )
+
+        def product(bank, codes, scales, s):
+            cols = slice(s * P, (s + 1) * P)
+            for d in range(D):
+                piece = slice(d * V, (d + 1) * V)
+                nc.tensor.matmul_mx(
+                    out=bank[:, d, :],
+                    lhsT=x_codes[:, piece].bitcast(FP8X4),
+                    lhsT_scale=x_scales[:, piece],
+                    rhs=codes[:, cols].bitcast(FP8X4),
+                    rhs_scale=scales[:, cols],
+                    start=True,
+                    stop=True,
+                )
+
+        def turn_and_sum(out, terms):
+            for d in range(D):
+                nc.tensor.matmul(
+                    out=out, lhsT=terms[:, d, :], rhs=ident[:], is_transpose=True, start=(d == 0), stop=(d == D - 1)
+                )
+
+        w1_grouped = keep.tile([P, N * PACK], BF16, name="w1_grouped", align_bytes=64)
+        w1_view = w1_grouped[:].rearrange("p (t m j) -> p m j t", t=PACK, j=PACK)
+        w1_source = w1_raw[:].rearrange("p j (m t) -> p m j t", t=PACK)
+        w1_codes = keep.tile([P, N], U32, name="w1_codes", align_bytes=64)
+        w1_scales = keep.tile([P, N], U8, name="w1_scales", align_bytes=64)
+        nc.scalar.activation(out=w1_view[:, :, :, 0:2], in_=w1_source[:, :, :, 0:2], func=ACT.Copy)
+        nc.vector.tensor_copy(out=w1_view[:, :, :, 2:4], in_=w1_source[:, :, :, 2:4])
+        score = []
+        for a, b in ((0, 2), (2, 4)):
+            quantize(w1_codes, w1_scales, w1_grouped, a * P, b * P)
+            for t in range(a, b):
+                bank = psum.tile([P, D, P], F32, name="score%d" % t, tag="score_bank%d" % t)
+                product(bank, w1_codes, w1_scales, t)
+                score.append(bank)
+
+        w2_grouped = keep.tile([P, N * PACK], BF16, name="w2_grouped", align_bytes=64)
+        w2_view = w2_grouped[:].rearrange("p (t m j) -> p m j t", t=PACK, j=PACK)
+        w2_source = w2_raw[:].rearrange("p j (m t) -> p m j t", t=PACK)
+        w2_codes = keep.tile([P, N], U32, name="w2_codes", align_bytes=64)
+        w2_scales = keep.tile([P, N], U8, name="w2_scales", align_bytes=64)
+        for c in range(2):
+            ms = slice(c * P // 2, (c + 1) * P // 2)
+            nc.scalar.activation(out=w2_view[:, ms], in_=w2_source[:, ms], func=ACT.Copy)
+
+        top = keep.tile([P, PACK, P], F32, name="top")
+        shifted = [keep.tile([P, D, P], F32, name="shifted%d" % s, tag="shifted%d" % s) for s in range(PACK)]
+        e = [keep.tile([P, D, P], F32, name="e%d" % t) for t in range(PACK)]
+        den_squared = keep.tile([P, PACK, V], F32, name="den_squared")
+        den = []
+        value = []
+
+        def largest(s):
+            nc.vector.tensor_reduce(
+                out=top[:, s, :], in_=score[s][:].rearrange("v d m -> v m d"), axis=AXIS.X, op=ALU.max
+            )
+
+        def weigh(t, pieces):
+            for a, b in pieces:
+                nc.vector.tensor_tensor(
+                    out=shifted[t][:, a:b, :],
+                    in0=score[t][:, a:b, :],
+                    in1=top[:, t : t + 1, :].to_broadcast([P, b - a, P]),
+                    op=ALU.subtract,
+                )
+                nc.scalar.activation(out=e[t][:, a:b, :], in_=shifted[t][:, a:b, :], func=ACT.Exp)
+            if t % 2 == 0:
+                den.append(psum.tile([P, 2, V], F32, name="den%d" % (t // 2), tag="score_bank%d" % t))
+            turn_and_sum(den[t // 2][:, t % 2, :], e[t])
+
+        whole = ((0, D),)
+        halves = ((0, D // 2), (D // 2, D))
+        largest(0)
+        largest(1)
+        weigh(0, whole)
+        largest(2)
+        weigh(1, whole)
+        nc.scalar.activation(out=den_squared[:, 0:2, :], in_=den[0][:], func=ACT.Square)
+        quantize(w2_codes, w2_scales, w2_grouped, 0, N)
+        for t in range(PACK):
+            bank = psum.tile([P, D, P], F32, name="value%d" % t, tag="value_bank%d" % t)
+            product(bank, w2_codes, w2_scales, t)
+            value.append(bank)
+        largest(3)
+        weigh(2, whole)
+        weigh(3, halves)
+
+        inverse = keep.tile([P, PACK, V], F32, name="inverse", tag="shifted3")
+        nc.scalar.activation(out=inverse[:, 0:2, :], in_=den_squared[:, 0:2, :], func=ACT.Abs_reciprocal_sqrt)
+        nc.scalar.activation(out=den_squared[:, 2:4, :], in_=den[1][:], func=ACT.Square)
+        nc.scalar.activation(out=inverse[:, 2:4, :], in_=den_squared[:, 2:4, :], func=ACT.Abs_reciprocal_sqrt)
+
+        weighted = [keep.tile([P, D, P], F32, name="weighted%d" % t) for t in range(PACK)]
+        num = []
+        for t in range(PACK):
+            u, i = divmod(t, 2)
+            for a, b in halves if t == PACK - 1 else whole:
+                nc.vector.tensor_tensor(
+                    out=weighted[t][:, a:b, :], in0=value[t][:, a:b, :], in1=e[t][:, a:b, :], op=ALU.mult
+                )
+            if i == 0:
+                num.append(psum.tile([P, 2, V], F32, name="num%d" % u, tag="score_bank%d" % (t + 1)))
+            turn_and_sum(num[u][:, i, :], weighted[t])
+
+        y_grouped = keep.tile([P, V, PACK], BF16, name="y_grouped", align_bytes=64)
+        out_rows = out_0.rearrange("(p t) v -> p t v", t=PACK)
+        for u in range(2):
+            pair = slice(2 * u, 2 * u + 2)
+            y = keep.tile([P, 2, V], F32, name="y%d" % u)
+            nc.vector.tensor_tensor(out=y[:], in0=num[u][:], in1=inverse[:, pair, :], op=ALU.mult)
+            nc.sync.dma_start(out=out_rows[:, pair, :], in_=y[:])
+            nc.vector.tensor_copy(out=y_grouped[:, :, pair], in_=y[:].rearrange("p t c -> p c t"))
+        y_codes = keep.tile([P, V], U32, name="y_codes", align_bytes=64)
+        y_scales = keep.tile([P, V], U8, name="y_scales", align_bytes=64)
+        quantize(y_codes, y_scales, y_grouped[:].rearrange("p c t -> p (c t)"), 0, V)
+        nc.sync.dma_start(out=out_1.rearrange("z l c r -> (z l) (c r)").bitcast(I32), in_=y_codes[:].bitcast(I32))
+        scale_rows = out_2.rearrange("z q c -> (z q) c").bitcast(I32)
+        for q in range(4):
+            queue = nc.scalar if q % 2 == 0 else nc.sync
+            queue.dma_start(out=scale_rows[4 * q : 4 * q + 4, :], in_=y_scales[32 * q : 32 * q + 4, :].bitcast(I32))

@@ -85,17 +85,20 @@ def tile_picked_apool_none_lo_kernel(tc, xT, w1, w2, offs, out_0, out_1, out_2):
                     out=out, lhsT=terms[:, d, :], rhs=ident[:], is_transpose=True, start=(d == 0), stop=(d == D - 1)
                 )
 
-        w1_grouped = keep.tile([P, N * PACK], BF16, name="w1_grouped", align_bytes=64)
-        w1_view = w1_grouped[:].rearrange("p (t m j) -> p m j t", t=PACK, j=PACK)
         w1_source = w1_raw[:].rearrange("p j (m t) -> p m j t", t=PACK)
         w1_codes = keep.tile([P, N], U32, name="w1_codes", align_bytes=64)
         w1_scales = keep.tile([P, N], U8, name="w1_scales", align_bytes=64)
-        nc.scalar.activation(out=w1_view[:, :, :, 0:2], in_=w1_source[:, :, :, 0:2], func=ACT.Copy)
-        nc.vector.tensor_copy(out=w1_view[:, :, :, 2:4], in_=w1_source[:, :, :, 2:4])
         score = []
-        for a, b in ((0, 2), (2, 4)):
-            quantize(w1_codes, w1_scales, w1_grouped, a * P, b * P)
-            for t in range(a, b):
+        for u in range(2):
+            grouped = keep.tile([P, 2 * P * PACK], BF16, name="w1_grouped%d" % u, tag="w1_grouped", align_bytes=64)
+            view = grouped[:].rearrange("p (t m j) -> p m j t", t=2, j=PACK)
+            if u == 0:
+                nc.scalar.activation(out=view, in_=w1_source[:, :, :, 0:2], func=ACT.Copy)
+            else:
+                nc.vector.tensor_copy(out=view, in_=w1_source[:, :, :, 2:4])
+            cols = slice(2 * u * P, 2 * (u + 1) * P)
+            nc.vector.quantize_mx(out=w1_codes[:, cols].bitcast(FP8X4), scales=w1_scales[:, cols], in_=grouped[:])
+            for t in range(2 * u, 2 * u + 2):
                 bank = psum.tile([P, D, P], F32, name="score%d" % t, tag="score_bank%d" % t)
                 product(bank, w1_codes, w1_scales, t)
                 score.append(bank)
@@ -134,6 +137,13 @@ def tile_picked_apool_none_lo_kernel(tc, xT, w1, w2, offs, out_0, out_1, out_2):
                 den.append(psum.tile([P, 2, V], F32, name="den%d" % (t // 2), tag="score_bank%d" % t))
             turn_and_sum(den[t // 2][:, t % 2, :], e[t])
 
+        def values(u):
+            quantize(w2_codes, w2_scales, w2_grouped, 2 * u * P, 2 * (u + 1) * P)
+            for t in range(2 * u, 2 * u + 2):
+                bank = psum.tile([P, D, P], F32, name="value%d" % t, tag="value_bank%d" % t)
+                product(bank, w2_codes, w2_scales, t)
+                value.append(bank)
+
         whole = ((0, D),)
         halves = ((0, D // 2), (D // 2, D))
         largest(0)
@@ -142,14 +152,11 @@ def tile_picked_apool_none_lo_kernel(tc, xT, w1, w2, offs, out_0, out_1, out_2):
         largest(2)
         weigh(1, whole)
         nc.scalar.activation(out=den_squared[:, 0:2, :], in_=den[0][:], func=ACT.Square)
-        quantize(w2_codes, w2_scales, w2_grouped, 0, N)
-        for t in range(PACK):
-            bank = psum.tile([P, D, P], F32, name="value%d" % t, tag="value_bank%d" % t)
-            product(bank, w2_codes, w2_scales, t)
-            value.append(bank)
+        values(0)
         largest(3)
         weigh(2, whole)
         weigh(3, halves)
+        values(1)
 
         inverse = keep.tile([P, PACK, V], F32, name="inverse", tag="shifted3")
         nc.scalar.activation(out=inverse[:, 0:2, :], in_=den_squared[:, 0:2, :], func=ACT.Abs_reciprocal_sqrt)
@@ -173,9 +180,14 @@ def tile_picked_apool_none_lo_kernel(tc, xT, w1, w2, offs, out_0, out_1, out_2):
         for u in range(2):
             pair = slice(2 * u, 2 * u + 2)
             y = keep.tile([P, 2, V], F32, name="y%d" % u)
+            nc.vector.tensor_tensor(
+                out=y_grouped[:, :, pair],
+                in0=num[u][:].rearrange("p t c -> p c t"),
+                in1=inverse[:, pair, :].rearrange("p t c -> p c t"),
+                op=ALU.mult,
+            )
             nc.vector.tensor_tensor(out=y[:], in0=num[u][:], in1=inverse[:, pair, :], op=ALU.mult)
             nc.sync.dma_start(out=out_rows[:, pair, :], in_=y[:])
-            nc.vector.tensor_copy(out=y_grouped[:, :, pair], in_=y[:].rearrange("p t c -> p c t"))
         y_codes = keep.tile([P, V], U32, name="y_codes", align_bytes=64)
         y_scales = keep.tile([P, V], U8, name="y_scales", align_bytes=64)
         quantize(y_codes, y_scales, y_grouped[:].rearrange("p c t -> p (c t)"), 0, V)

@@ -38,8 +38,10 @@ def tile_picked_apool_none_lo_kernel(tc, xT, w1, w2, offs, out_0, out_1, out_2):
 
         w1_raw = keep.tile([P, PACK, N], F32, name="w1_raw")
         nc.sync.dma_start(out=w1_raw[:], in_=w1.rearrange("(p j) n -> p j n", j=PACK))
-        w2_raw = keep.tile([P, PACK, N], F32, name="w2_raw")
-        nc.sync.dma_start(out=w2_raw[:], in_=w2.rearrange("(p j) n -> p j n", j=PACK))
+        w2_rows = w2.rearrange("(p j) n -> p j n", j=PACK)
+        w2_raw = [keep.tile([P, PACK, N // 2], F32, name="w2_raw%d" % c, tag="w2_raw%d" % c) for c in range(2)]
+        for c in range(2):
+            nc.sync.dma_start(out=w2_raw[c][:], in_=w2_rows[:, :, c * N // 2 : (c + 1) * N // 2])
 
         ident = keep.tile([P, P], F32, name="ident")
         make_identity(nc, ident[:])
@@ -80,9 +82,10 @@ def tile_picked_apool_none_lo_kernel(tc, xT, w1, w2, offs, out_0, out_1, out_2):
                 )
 
         def turn_and_sum(out, terms):
-            for d in range(D):
+            count = terms.shape[1]
+            for d in range(count):
                 nc.tensor.matmul(
-                    out=out, lhsT=terms[:, d, :], rhs=ident[:], is_transpose=True, start=(d == 0), stop=(d == D - 1)
+                    out=out, lhsT=terms[:, d, :], rhs=ident[:], is_transpose=True, start=(d == 0), stop=(d == count - 1)
                 )
 
         w1_source = w1_raw[:].rearrange("p j (m t) -> p m j t", t=PACK)
@@ -103,65 +106,76 @@ def tile_picked_apool_none_lo_kernel(tc, xT, w1, w2, offs, out_0, out_1, out_2):
                 product(bank, w1_codes, w1_scales, t)
                 score.append(bank)
 
-        w2_grouped = keep.tile([P, N * PACK], BF16, name="w2_grouped", align_bytes=64)
+        w2_grouped = keep.tile([P, N * PACK], BF16, name="w2_grouped", tag="w2_grouped", align_bytes=64)
         w2_view = w2_grouped[:].rearrange("p (t m j) -> p m j t", t=PACK, j=PACK)
-        w2_source = w2_raw[:].rearrange("p j (m t) -> p m j t", t=PACK)
         w2_codes = keep.tile([P, N], U32, name="w2_codes", align_bytes=64)
         w2_scales = keep.tile([P, N], U8, name="w2_scales", align_bytes=64)
-        for c in range(2):
-            ms = slice(c * P // 2, (c + 1) * P // 2)
-            nc.scalar.activation(out=w2_view[:, ms], in_=w2_source[:, ms], func=ACT.Copy)
 
-        top = keep.tile([P, PACK, P], F32, name="top")
+        def round_w2(c):
+            nc.scalar.activation(
+                out=w2_view[:, c * P // 2 : (c + 1) * P // 2],
+                in_=w2_raw[c][:].rearrange("p j (m t) -> p m j t", t=PACK),
+                func=ACT.Copy,
+            )
+
+        top = []
         shifted = [keep.tile([P, D, P], F32, name="shifted%d" % s, tag="shifted%d" % s) for s in range(PACK)]
-        e = [keep.tile([P, D, P], F32, name="e%d" % t) for t in range(PACK)]
+        e = []
         den_squared = keep.tile([P, PACK, V], F32, name="den_squared")
         den = []
+        pairs = {}
         value = []
 
         def largest(s):
+            if s % 2 == 0:
+                tag = "top" if s == 0 else "w2_grouped"
+                top.append(keep.tile([P, 2, P], F32, name="top%d" % (s // 2), tag=tag, align_bytes=64))
             nc.vector.tensor_reduce(
-                out=top[:, s, :], in_=score[s][:].rearrange("v d m -> v m d"), axis=AXIS.X, op=ALU.max
+                out=top[s // 2][:, s % 2, :], in_=score[s][:].rearrange("v d m -> v m d"), axis=AXIS.X, op=ALU.max
             )
 
         def weigh(t, pieces):
+            e.append(keep.tile([P, D, P], F32, name="e%d" % t, tag="w2_raw1" if t == 0 else "e%d" % t))
             for a, b in pieces:
                 nc.vector.tensor_tensor(
                     out=shifted[t][:, a:b, :],
                     in0=score[t][:, a:b, :],
-                    in1=top[:, t : t + 1, :].to_broadcast([P, b - a, P]),
+                    in1=top[t // 2][:, t % 2 : t % 2 + 1, :].to_broadcast([P, b - a, P]),
                     op=ALU.subtract,
                 )
                 nc.scalar.activation(out=e[t][:, a:b, :], in_=shifted[t][:, a:b, :], func=ACT.Exp)
-            if t % 2 == 0:
-                den.append(psum.tile([P, 2, V], F32, name="den%d" % (t // 2), tag="score_bank%d" % t))
-            turn_and_sum(den[t // 2][:, t % 2, :], e[t])
+            if t == 0:
+                den.append(psum.tile([P, 2, V], F32, name="den0", tag="score_bank0"))
+            if t < 2:
+                turn_and_sum(den[0][:, t, :], e[t])
+            else:
+                pairs[t] = keep.tile([P, 2, P], F32, name="pairs%d" % t)
+                nc.gpsimd.tensor_tensor(out=pairs[t][:], in0=e[t][:, 0:2, :], in1=e[t][:, 2:4, :], op=ALU.add)
 
-        def values(u):
-            quantize(w2_codes, w2_scales, w2_grouped, 2 * u * P, 2 * (u + 1) * P)
-            for t in range(2 * u, 2 * u + 2):
+        def values():
+            quantize(w2_codes, w2_scales, w2_grouped, 0, N)
+            for t in range(PACK):
                 bank = psum.tile([P, D, P], F32, name="value%d" % t, tag="value_bank%d" % t)
                 product(bank, w2_codes, w2_scales, t)
                 value.append(bank)
 
         whole = ((0, D),)
         halves = ((0, D // 2), (D // 2, D))
+        round_w2(0)
+        round_w2(1)
         largest(0)
         largest(1)
         weigh(0, whole)
-        largest(2)
         weigh(1, whole)
         nc.scalar.activation(out=den_squared[:, 0:2, :], in_=den[0][:], func=ACT.Square)
-        values(0)
+        values()
+        largest(2)
         largest(3)
-        weigh(2, whole)
+        weigh(2, halves)
         weigh(3, halves)
-        values(1)
 
         inverse = keep.tile([P, PACK, V], F32, name="inverse", tag="shifted3")
         nc.scalar.activation(out=inverse[:, 0:2, :], in_=den_squared[:, 0:2, :], func=ACT.Abs_reciprocal_sqrt)
-        nc.scalar.activation(out=den_squared[:, 2:4, :], in_=den[1][:], func=ACT.Square)
-        nc.scalar.activation(out=inverse[:, 2:4, :], in_=den_squared[:, 2:4, :], func=ACT.Abs_reciprocal_sqrt)
 
         weighted = [keep.tile([P, D, P], F32, name="weighted%d" % t) for t in range(PACK)]
         num = []
@@ -174,6 +188,12 @@ def tile_picked_apool_none_lo_kernel(tc, xT, w1, w2, offs, out_0, out_1, out_2):
             if i == 0:
                 num.append(psum.tile([P, 2, V], F32, name="num%d" % u, tag="score_bank%d" % (t + 1)))
             turn_and_sum(num[u][:, i, :], weighted[t])
+            if t == 1:
+                den.append(psum.tile([P, 2, V], F32, name="den1", tag="value_bank1"))
+                for i in range(2):
+                    turn_and_sum(den[1][:, i, :], pairs[2 + i])
+        nc.scalar.activation(out=den_squared[:, 2:4, :], in_=den[1][:], func=ACT.Square)
+        nc.scalar.activation(out=inverse[:, 2:4, :], in_=den_squared[:, 2:4, :], func=ACT.Abs_reciprocal_sqrt)
 
         y_grouped = keep.tile([P, V, PACK], BF16, name="y_grouped", align_bytes=64)
         out_rows = out_0.rearrange("(p t) v -> p t v", t=PACK)

from contextlib import ExitStack

import concourse.mybir as mybir
from concourse.masks import make_identity

K, T, S, V, N = 512, 1024, 512, 128, 512
D = S // V
P = 128
PACK = 4

FLOPS = 2 * 2 * K * N * S

F32 = mybir.dt.float32
BF16 = mybir.dt.bfloat16
I32 = mybir.dt.int32
U32 = mybir.dt.uint32
U16 = mybir.dt.uint16
U8 = mybir.dt.uint8
FP8X4 = mybir.dt.float8_e4m3fn_x4
ACT = mybir.ActivationFunctionType
ALU = mybir.AluOpType
AXIS = mybir.AxisListType


def tile_picked_apool_none_lo_kernel(tc, xT, w1, w2, offs, out_0, out_1, out_2):
    nc = tc.nc
    with ExitStack() as ctx:
        keep = ctx.enter_context(tc.tile_pool(name="keep", bufs=1))
        psum = ctx.enter_context(tc.psum_pool(name="psum", bufs=1))

        offsets = keep.tile([P, S // 16], U16, name="offsets")
        x_rows = xT.rearrange("(p j) t -> p j t", j=PACK)
        x_plane = [keep.tile([P, T], F32, name="x_plane%d" % j) for j in range(PACK)]
        nc.sync.dma_start(out=x_plane[0][:], in_=x_rows[:, 0, :])
        nc.sync.dma_start(offsets[:], offs)
        for j in range(1, PACK):
            nc.sync.dma_start(out=x_plane[j][:], in_=x_rows[:, j, :])

        w1_raw = keep.tile([P, PACK, N], F32, name="w1_raw")
        nc.sync.dma_start(out=w1_raw[:], in_=w1.rearrange("(p j) n -> p j n", j=PACK))
        w2_rows = w2.rearrange("(p j) n -> p j n", j=PACK)
        w2_raw = [keep.tile([P, PACK, N // 2], F32, name="w2_raw%d" % c, tag="w2_raw%d" % c) for c in range(2)]
        for c in range(2):
            nc.sync.dma_start(out=w2_raw[c][:], in_=w2_rows[:, :, c * N // 2 : (c + 1) * N // 2])

        ident = keep.tile([P, P], F32, name="ident")
        make_identity(nc, ident[:])

        picked = keep.tile([P, PACK, S], BF16, name="picked")
        for j in range(PACK):
            nc.vector.tensor_copy(picked[:, j, :], x_plane[j][:].indirect(offsets[:]))
        x_grouped = keep.tile([P, S, PACK], BF16, name="x_grouped", align_bytes=64)
        nc.scalar.activation(
            out=x_grouped[:, :, 0:2],
            in_=picked[:, 0:2, :].rearrange("p j c -> p c j"),
            func=ACT.Copy,
        )
        nc.vector.tensor_copy(out=x_grouped[:, :, 2:4], in_=picked[:, 2:4, :].rearrange("p j c -> p c j"))
        x_codes = keep.tile([P, S], U32, name="x_codes", align_bytes=64)
        x_scales = keep.tile([P, S], U8, name="x_scales", align_bytes=64)
        nc.vector.quantize_mx(
            out=x_codes[:].bitcast(FP8X4), scales=x_scales[:], in_=x_grouped[:].rearrange("p c j -> p (c j)")
        )

        def quantize(codes, scales, grouped, a, b):
            nc.vector.quantize_mx(
                out=codes[:, a:b].bitcast(FP8X4), scales=scales[:, a:b], in_=grouped[:, a * PACK : b * PACK]
            )

        def product(bank, codes, scales, s):
            cols = slice(s * P, (s + 1) * P)
            for d in range(D):
                piece = slice(d * V, (d + 1) * V)
                nc.tensor.matmul_mx(
                    out=bank[:, d, :],
                    lhsT=x_codes[:, piece].bitcast(FP8X4),
                    lhsT_scale=x_scales[:, piece],
                    rhs=codes[:, cols].bitcast(FP8X4),
                    rhs_scale=scales[:, cols],
                    start=True,
                    stop=True,
                )

        def turn_and_sum(out, terms):
            count = terms.shape[1]
            for d in range(count):
                nc.tensor.matmul(
                    out=out, lhsT=terms[:, d, :], rhs=ident[:], is_transpose=True, start=(d == 0), stop=(d == count - 1)
                )

        w1_source = w1_raw[:].rearrange("p j (m t) -> p m j t", t=PACK)
        w1_codes = keep.tile([P, N], U32, name="w1_codes", align_bytes=64)
        w1_scales = keep.tile([P, N], U8, name="w1_scales", align_bytes=64)
        score = []
        for u in range(2):
            grouped = keep.tile([P, 2 * P * PACK], BF16, name="w1_grouped%d" % u, tag="w1_grouped", align_bytes=64)
            view = grouped[:].rearrange("p (t m j) -> p m j t", t=2, j=PACK)
            if u == 0:
                nc.scalar.activation(out=view, in_=w1_source[:, :, :, 0:2], func=ACT.Copy)
            else:
                nc.vector.tensor_copy(out=view, in_=w1_source[:, :, :, 2:4])
            cols = slice(2 * u * P, 2 * (u + 1) * P)
            nc.vector.quantize_mx(out=w1_codes[:, cols].bitcast(FP8X4), scales=w1_scales[:, cols], in_=grouped[:])
            for t in range(2 * u, 2 * u + 2):
                bank = psum.tile([P, D, P], F32, name="score%d" % t, tag="score_bank%d" % t)
                product(bank, w1_codes, w1_scales, t)
                score.append(bank)

        w2_grouped = keep.tile([P, N * PACK], BF16, name="w2_grouped", tag="w2_grouped", align_bytes=64)
        w2_view = w2_grouped[:].rearrange("p (t m j) -> p m j t", t=PACK, j=PACK)
        w2_codes = keep.tile([P, N], U32, name="w2_codes", align_bytes=64)
        w2_scales = keep.tile([P, N], U8, name="w2_scales", align_bytes=64)

        def round_w2(c):
            nc.scalar.activation(
                out=w2_view[:, c * P // 2 : (c + 1) * P // 2],
                in_=w2_raw[c][:].rearrange("p j (m t) -> p m j t", t=PACK),
                func=ACT.Copy,
            )

        top = []
        shifted = [keep.tile([P, D, P], F32, name="shifted%d" % s, tag="shifted%d" % s) for s in range(PACK)]
        e = []
        den_squared = keep.tile([P, PACK, V], F32, name="den_squared")
        den = []
        pairs = {}
        value = []

        def largest(s):
            if s % 2 == 0:
                tag = "top" if s == 0 else "w2_grouped"
                top.append(keep.tile([P, 2, P], F32, name="top%d" % (s // 2), tag=tag, align_bytes=64))
            nc.vector.tensor_reduce(
                out=top[s // 2][:, s % 2, :], in_=score[s][:].rearrange("v d m -> v m d"), axis=AXIS.X, op=ALU.max
            )

        def weigh(t, pieces):
            e.append(keep.tile([P, D, P], F32, name="e%d" % t, tag="w2_raw1" if t == 0 else "e%d" % t))
            for a, b in pieces:
                nc.vector.tensor_tensor(
                    out=shifted[t][:, a:b, :],
                    in0=score[t][:, a:b, :],
                    in1=top[t // 2][:, t % 2 : t % 2 + 1, :].to_broadcast([P, b - a, P]),
                    op=ALU.subtract,
                )
                nc.scalar.activation(out=e[t][:, a:b, :], in_=shifted[t][:, a:b, :], func=ACT.Exp)
            if t == 0:
                den.append(psum.tile([P, 2, V], F32, name="den0", tag="score_bank0"))
            if t < 2:
                turn_and_sum(den[0][:, t, :], e[t])
            else:
                pairs[t] = keep.tile([P, 2, P], F32, name="pairs%d" % t)
                nc.gpsimd.tensor_tensor(out=pairs[t][:], in0=e[t][:, 0:2, :], in1=e[t][:, 2:4, :], op=ALU.add)

        def values():
            quantize(w2_codes, w2_scales, w2_grouped, 0, N)
            for t in range(PACK):
                bank = psum.tile([P, D, P], F32, name="value%d" % t, tag="value_bank%d" % t)
                product(bank, w2_codes, w2_scales, t)
                value.append(bank)

        whole = ((0, D),)
        halves = ((0, D // 2), (D // 2, D))
        round_w2(0)
        round_w2(1)
        largest(0)
        largest(1)
        weigh(0, whole)
        weigh(1, whole)
        nc.scalar.activation(out=den_squared[:, 0:2, :], in_=den[0][:], func=ACT.Square)
        values()
        largest(2)
        largest(3)
        weigh(2, halves)
        weigh(3, halves)

        inverse = keep.tile([P, PACK, V], F32, name="inverse", tag="shifted3")
        nc.scalar.activation(out=inverse[:, 0:2, :], in_=den_squared[:, 0:2, :], func=ACT.Abs_reciprocal_sqrt)

        weighted = [keep.tile([P, D, P], F32, name="weighted%d" % t) for t in range(PACK)]
        num = []
        for t in range(PACK):
            u, i = divmod(t, 2)
            for a, b in halves if t == PACK - 1 else whole:
                nc.vector.tensor_tensor(
                    out=weighted[t][:, a:b, :], in0=value[t][:, a:b, :], in1=e[t][:, a:b, :], op=ALU.mult
                )
            if i == 0:
                num.append(psum.tile([P, 2, V], F32, name="num%d" % u, tag="score_bank%d" % (t + 1)))
            turn_and_sum(num[u][:, i, :], weighted[t])
            if t == 1:
                den.append(psum.tile([P, 2, V], F32, name="den1", tag="value_bank1"))
                for i in range(2):
                    turn_and_sum(den[1][:, i, :], pairs[2 + i])
        nc.scalar.activation(out=den_squared[:, 2:4, :], in_=den[1][:], func=ACT.Square)
        nc.scalar.activation(out=inverse[:, 2:4, :], in_=den_squared[:, 2:4, :], func=ACT.Abs_reciprocal_sqrt)

        y_grouped = keep.tile([P, V, PACK], BF16, name="y_grouped", align_bytes=64)
        out_rows = out_0.rearrange("(p t) v -> p t v", t=PACK)
        for u in range(2):
            pair = slice(2 * u, 2 * u + 2)
            y = keep.tile([P, 2, V], F32, name="y%d" % u)
            nc.vector.tensor_tensor(
                out=y_grouped[:, :, pair],
                in0=num[u][:].rearrange("p t c -> p c t"),
                in1=inverse[:, pair, :].rearrange("p t c -> p c t"),
                op=ALU.mult,
            )
            nc.vector.tensor_tensor(out=y[:], in0=num[u][:], in1=inverse[:, pair, :], op=ALU.mult)
            nc.sync.dma_start(out=out_rows[:, pair, :], in_=y[:])
        y_codes = keep.tile([P, V], U32, name="y_codes", align_bytes=64)
        y_scales = keep.tile([P, V], U8, name="y_scales", align_bytes=64)
        quantize(y_codes, y_scales, y_grouped[:].rearrange("p c t -> p (c t)"), 0, V)
        nc.sync.dma_start(out=out_1.rearrange("z l c r -> (z l) (c r)").bitcast(I32), in_=y_codes[:].bitcast(I32))
        scale_rows = out_2.rearrange("z q c -> (z q) c").bitcast(I32)
        for q in range(4):
            queue = nc.scalar if q % 2 == 0 else nc.sync
            queue.dma_start(out=scale_rows[4 * q : 4 * q + 4, :], in_=y_scales[32 * q : 32 * q + 4, :].bitcast(I32))
